import numpy as np
import ml_dtypes


def mxq(x, axis, fmt="e4m3"):
    dtype, down = {"e4m3": (ml_dtypes.float8_e4m3fn, 7), "e5m2": (ml_dtypes.float8_e5m2, 14)}[fmt]
    v = np.moveaxis(np.asarray(x, np.float32).astype(ml_dtypes.bfloat16).astype(np.float64), axis, -1)
    blocks = v.reshape(v.shape[:-1] + (-1, 32))
    amax = np.abs(blocks).max(-1, keepdims=True)
    byte = np.maximum(np.where(amax > 0, np.frexp(amax)[1] - 1 + 127, 0) - down, 1)
    scale = np.exp2(byte - 127.0)
    codes = (blocks / scale).astype(np.float32).astype(dtype).astype(np.float64)
    return np.moveaxis((codes * scale).reshape(v.shape), -1, axis)


WIDE = False


def mx_kscale(k):
    if not WIDE:
        return np.ones(k)
    levels = np.array([10, -10, 5, -5, 0])
    if k % 512:
        return np.exp2(np.random.permutation(np.resize(levels, k // 32))).repeat(32)
    a = np.empty((k // 512, 16))
    for p in range(k // 512):
        a[p, :8] = np.random.permutation(np.resize(levels, 8))
        for g in range(8):
            far = levels[np.abs(levels - a[p, g]) >= 10]
            a[p, g + 8] = far[np.random.randint(len(far))]
    return np.exp2(a.ravel()).repeat(32)


def f64(x):
    return np.asarray(x).astype(np.float64)


def striped8(idx):
    return np.asarray(idx).reshape(8, -1, 16).transpose(0, 2, 1).reshape(128, -1).astype(np.uint16)


def unstriped8(offs):
    return offs.reshape(8, 16, -1).transpose(0, 2, 1).reshape(8, -1).astype(np.int64)


def pick8(x, idx, run):
    r = np.arange(len(x))
    return x[r[:, None], idx[r % (8 * run) // run]]


E2M1 = np.array([0.0, 0.5, 1.0, 1.5, 2.0, 3.0, 4.0, 6.0, -0.0, -0.5, -1.0, -1.5, -2.0, -3.0, -4.0, -6.0])


def pack_weight(w, fmt):
    k, n = w.shape
    w = f64(np.asarray(w, np.float32).astype(ml_dtypes.bfloat16)).reshape(k // 32, 32, n)
    amax = np.abs(w).max(1)
    if fmt == "e4m3":
        byte = np.frexp(amax)[1] - 1 + 127 - 7
    else:
        mant, ex = np.frexp(amax / 6.0)
        byte = np.where(mant > 0.5, ex, ex - 1) + 127
    byte = np.clip(np.where(amax > 0, byte, 1), 1, 254)
    scaled = (w * np.exp2(127.0 - byte)[:, None, :]).reshape(k, n).astype(np.float32)
    by_word = np.ascontiguousarray(scaled.reshape(k // 512, 128, 4, n).transpose(0, 1, 3, 2))
    if fmt == "e4m3":
        words = by_word.astype(ml_dtypes.float8_e4m3fn).view(np.uint8)
    else:
        c = by_word.astype(ml_dtypes.float4_e2m1fn).view(np.uint8) & 0xF
        words = (c[..., 0::2] | (c[..., 1::2] << 4)).reshape(k // 512, 128, 2 * n)
    return np.ascontiguousarray(words), np.ascontiguousarray(byte.astype(np.uint8).reshape(k // 512, 16, n))


def unpack_weight(words, scales, fmt):
    g, _, n = scales.shape
    words = np.ascontiguousarray(words).reshape(g, 128, n, -1)
    if fmt == "e4m3":
        vals = words.view(ml_dtypes.float8_e4m3fn).astype(np.float64)
    else:
        nib = np.empty((g, 128, n, 4), np.uint8)
        nib[..., 0::2] = words & 0xF
        nib[..., 1::2] = words >> 4
        vals = E2M1[nib]
    vals = vals * np.repeat(np.exp2(scales.astype(np.float64) - 127.0), 8, axis=1)[..., None]
    return vals.transpose(0, 1, 3, 2).reshape(g * 512, n)


D, T, U, X, I, Q = 512, 1024, 1024, 1024, 512, 128


def setup_inputs():
    n = np.random.standard_normal
    idx = np.stack([np.random.permutation(T)[:I] for _ in range(8)])
    idx2 = np.stack([np.random.permutation(U)[:I] for _ in range(8)])
    idx3 = np.stack([np.random.permutation(X)[:I] for _ in range(8)])
    idx4 = np.stack([np.random.permutation(U)[:I] for _ in range(8)])
    idx5 = np.stack([np.random.permutation(U)[:I] for _ in range(8)])
    idx6 = np.stack([np.random.permutation(X)[:I] for _ in range(8)])
    fd = mx_kscale(D)
    keysp = pack_weight(n((D, T)) / fd[:, None], "e4m3")
    notesp = pack_weight(n((D, U)) / fd[:, None], "e2m1")
    usersp = pack_weight(n((D, X)) / fd[:, None], "e4m3")
    return {
        "query": (n((D, Q)) * 1.0 / np.sqrt(D) * fd[:, None]).astype(np.float32),
        "keys_words": keysp[0],
        "keys_scales": keysp[1],
        "notes_words": notesp[0],
        "notes_scales": notesp[1],
        "users_words": usersp[0],
        "users_scales": usersp[1],
        "offs": striped8(idx),
        "offs2": striped8(idx2),
        "offs3": striped8(idx3),
        "offs4": striped8(idx4),
        "offs5": striped8(idx5),
        "offs6": striped8(idx6),
    }


def reference(query, keys_words, keys_scales, notes_words, notes_scales, users_words, users_scales, offs, offs2, offs3, offs4, offs5, offs6):
    idx = unstriped8(offs)
    idx2 = unstriped8(offs2)
    idx3 = unstriped8(offs3)
    idx4 = unstriped8(offs4)
    idx5 = unstriped8(offs5)
    idx6 = unstriped8(offs6)
    keysu = unpack_weight(keys_words, keys_scales, "e4m3")
    notesu = unpack_weight(notes_words, notes_scales, "e2m1")
    usersu = unpack_weight(users_words, users_scales, "e4m3")
    queryq = mxq(f64(query), 0, "e4m3")
    a = queryq.T @ keysu
    b = queryq.T @ notesu
    c0 = queryq.T @ usersu
    w = pick8(a, idx, 16) - pick8(b, idx2, 16)
    v = pick8(c0, idx3, 16) - pick8(a, idx, 16)
    f1 = np.zeros((Q, X))
    f1[np.arange(Q)[:, None], idx3[np.arange(Q) % 128 // 16]] = w
    f2 = np.zeros((Q, U))
    f2[np.arange(Q)[:, None], idx4[np.arange(Q) % 128 // 16]] = v
    bb = b + f2
    cc = c0 + f1
    y = np.maximum(pick8(bb, idx5, 16), pick8(cc, idx6, 16))
    return y

@@ -1,0 +1,159 @@
+from contextlib import ExitStack
+
+import concourse.mybir as mybir
+from concourse.masks import make_identity
+
+F32 = mybir.dt.float32
+BF16 = mybir.dt.bfloat16
+I32 = mybir.dt.int32
+U32 = mybir.dt.uint32
+U16 = mybir.dt.uint16
+U8 = mybir.dt.uint8
+FP8X4 = mybir.dt.float8_e4m3fn_x4
+FP4X4 = mybir.dt.float4_e2m1fn_x4
+ADD = mybir.AluOpType.add
+MULT = mybir.AluOpType.mult
+MAX = mybir.AluOpType.max
+COPY = mybir.ActivationFunctionType.Copy
+
+P = 128
+D, POOL, SLOTS, Q = 512, 1024, 512, 128
+BANK = 512
+HALF = SLOTS // 2
+LIST_COLS = SLOTS // 16
+FLOPS = 3 * 2 * D * Q * POOL
+
+
+def tile_attend_twoerrands_three_kernel(tc, query, keys_words, keys_scales, notes_words, notes_scales, users_words,
+                                         users_scales, offs, offs2, offs3, offs4, offs5, offs6, out):
+    nc = tc.nc
+    with ExitStack() as ctx:
+        lists = ctx.enter_context(tc.tile_pool(name="lists", bufs=1))
+        sb = ctx.enter_context(tc.tile_pool(name="sb", bufs=1))
+        ps = ctx.enter_context(tc.psum_pool(name="ps", bufs=1))
+
+        def new_plane(name):
+            plane = sb.tile([P, POOL], U8, name=name, align_bytes=64)
+            nc.vector.memset(plane[:].bitcast(U32), 0)
+            return plane
+
+        def load_plane(plane, scales):
+            rows = scales[0].bitcast(I32)
+            for r in range(4):
+                nc.sync.dma_start(out=plane[r:P:32, :].bitcast(I32), in_=rows[r:16:4, :])
+
+        def load_list(name, src):
+            t = lists.tile([P, LIST_COLS], U16, name=name)
+            nc.sync.dma_start(t[:], src)
+            return t
+
+        n_plane = new_plane("n_plane")
+        k_plane = new_plane("k_plane")
+        u_plane = new_plane("u_plane")
+
+        q_raw = sb.tile([P, 4, Q], F32, name="q_raw")
+        nc.sync.dma_start(out=q_raw[:], in_=query.rearrange("(p j) q -> p j q", j=4))
+        l2 = load_list("l2", offs2)
+        load_plane(n_plane, notes_scales)
+        n_words = sb.tile([P, 2 * POOL], U8, name="n_words", align_bytes=64)
+        nc.sync.dma_start(out=n_words[:].bitcast(I32), in_=notes_words[0].bitcast(I32))
+        k_words = sb.tile([P, POOL], U32, name="k_words", align_bytes=64)
+        nc.sync.dma_start(out=k_words[:].bitcast(I32), in_=keys_words[0].rearrange("p n t -> p (n t)").bitcast(I32))
+        load_plane(k_plane, keys_scales)
+        u_words = sb.tile([P, POOL], U32, name="u_words", align_bytes=64)
+        nc.sync.dma_start(out=u_words[:].bitcast(I32), in_=users_words[0].rearrange("p n t -> p (n t)").bitcast(I32))
+        l1 = load_list("l1", offs)
+        load_plane(u_plane, users_scales)
+        l3 = load_list("l3", offs3)
+        l4 = load_list("l4", offs4)
+        l6 = load_list("l6", offs6)
+        l5 = load_list("l5", offs5)
+
+        f1 = sb.tile([P, POOL], F32, name="f1")
+        f2 = sb.tile([P, POOL], F32, name="f2")
+        nc.vector.memset(f1[:], 0.0)
+        nc.vector.memset(f2[:], 0.0)
+        ident = sb.tile([P, P], F32, name="ident")
+        make_identity(nc, ident[:])
+
+        q_bf = sb.tile([P, Q, 4], BF16, name="q_bf", align_bytes=64)
+        nc.vector.tensor_copy(out=q_bf[:].rearrange("p (c i) t -> p c t i", i=4),
+                              in_=q_raw[:].rearrange("p t (c i) -> p c t i", i=4))
+        q_codes = sb.tile([P, Q], U32, name="q_codes", align_bytes=64)
+        q_plane = sb.tile([P, Q], U8, name="q_plane", align_bytes=64)
+        nc.vector.quantize_mx(out=q_codes[:].bitcast(FP8X4), scales=q_plane[:], in_=q_bf[:].rearrange("p q t -> p (q t)"))
+
+        def score(tag, words, bytes_per_col, dtype, plane, x0, x1):
+            bank = ps.tile([P, x1 - x0], F32, name=tag)
+            nc.tensor.matmul_mx(out=bank[:], lhsT=q_codes[:].bitcast(FP8X4), lhsT_scale=q_plane[:],
+                                rhs=words[:, bytes_per_col * x0:bytes_per_col * x1].bitcast(dtype),
+                                rhs_scale=plane[:, x0:x1], start=True, stop=True)
+            return bank
+
+        def cols(h):
+            return slice(h * BANK, (h + 1) * BANK)
+
+        a = sb.tile([P, POOL], F32, name="a")
+        b = sb.tile([P, POOL], F32, name="b")
+        c0 = sb.tile([P, POOL], F32, name="c0")
+        b_cuts = (0, 512, 768, 1024)
+        b_ps = [score("b%d" % h, n_words, 2, FP4X4, n_plane, b_cuts[h], b_cuts[h + 1]) for h in range(3)]
+        a_ps = [score("a%d" % h, k_words, 1, FP8X4, k_plane, h * BANK, (h + 1) * BANK) for h in range(2)]
+        c_ps = [score("c%d" % h, u_words, 1, FP8X4, u_plane, h * BANK, (h + 1) * BANK) for h in range(2)]
+
+        hc = LIST_COLS // 2
+        nc.vector.tensor_copy(out=b[:, 0:512], in_=b_ps[0][:])
+        nc.scalar.activation(b[:, 512:768], b_ps[1][:], COPY)
+        nc.vector.tensor_copy(out=b[:, 768:1024], in_=b_ps[2][:])
+        neg_b = sb.tile([P, SLOTS], F32, name="neg_b")
+        nc.vector.tensor_scalar(neg_b[:, :HALF], b[:].indirect(l2[:, :hc]), -1.0, 0.0, MULT, ADD)
+        nc.scalar.activation(neg_b[:, HALF:], b[:].indirect(l2[:, hc:]), COPY, scale=-1.0)
+        nc.vector.tensor_copy(out=a[:, cols(0)], in_=a_ps[0][:])
+        nc.scalar.activation(a[:, cols(1)], a_ps[1][:], COPY)
+        a_at = sb.tile([P, SLOTS], F32, name="a_at")
+        nc.vector.tensor_copy(out=a_at[:, :HALF], in_=a[:].indirect(l1[:, :hc]))
+        nc.scalar.activation(a_at[:, HALF:], a[:].indirect(l1[:, hc:]), COPY)
+        nc.vector.tensor_tensor(f1[:].indirect(l3[:]), a_at[:], neg_b[:], ADD)
+
+        neg_a = sb.tile([P, SLOTS], F32, name="neg_a")
+        for h in range(2):
+            nc.scalar.activation(c0[:, cols(h)], c_ps[h][:], COPY)
+        nc.scalar.activation(neg_a[:], a_at[:], COPY, scale=-1.0)
+        c_at = sb.tile([P, SLOTS], F32, name="c_at")
+        nc.scalar.activation(c_at[:], c0[:].indirect(l3[:]), COPY)
+        nc.vector.tensor_tensor(f2[:].indirect(l4[:]), c_at[:], neg_a[:], ADD)
+
+        turned = [ps.tile([P, BANK], F32, name="a%d" % h) for h in range(2)]
+        for h in range(2):
+            for j in range(4):
+                x0 = h * BANK + j * P
+                nc.tensor.matmul(turned[h][:, j * P:(j + 1) * P], c0[:, x0:x0 + P], ident[:], start=(j == 0), stop=False,
+                                 is_transpose=True)
+        cc_t = sb.tile([P, POOL], F32, name="cc_t")
+        for h in range(2):
+            for j in range(4):
+                x0 = h * BANK + j * P
+                nc.tensor.matmul(turned[h][:, j * P:(j + 1) * P], f1[:, x0:x0 + P], ident[:], start=False, stop=(j == 3),
+                                 is_transpose=True)
+            nc.scalar.activation(cc_t[:, cols(h)], turned[h][:], COPY)
+        cc = sb.tile([P, POOL], F32, name="cc")
+        for h in range(2):
+            back = ps.tile([P, BANK], F32, name="c%d" % h)
+            for j in range(4):
+                x0 = h * BANK + j * P
+                nc.tensor.transpose(back[:, j * P:(j + 1) * P], cc_t[:, x0:x0 + P], ident[:])
+            nc.scalar.activation(cc[:, cols(h)], back[:], COPY)
+        cc_at = sb.tile([P, SLOTS], F32, name="cc_at")
+        nc.scalar.activation(cc_at[:], cc[:].indirect(l6[:]), COPY)
+
+        bb = sb.tile([P, POOL], F32, name="bb")
+        nc.vector.tensor_tensor(bb[:], b[:], f2[:], ADD)
+        bb_lo = sb.tile([P, HALF], F32, name="bb_lo")
+        bb_hi = sb.tile([P, HALF], F32, name="cc")
+        nc.vector.tensor_copy(out=bb_lo[:], in_=bb[:].indirect(l5[:, :hc]))
+        nc.scalar.activation(bb_hi[:], bb[:].indirect(l5[:, hc:]), COPY)
+        y = sb.tile([P, SLOTS], F32, name="y")
+        for h in range(2):
+            s = slice(h * HALF, (h + 1) * HALF)
+            nc.vector.tensor_tensor(y[:, s], (bb_lo, bb_hi)[h][:], cc_at[:, s], MAX)
+            nc.sync.dma_start(out=out[:, s], in_=y[:, s])

@@ -70,18 +70,23 @@ def tile_attend_twoerrands_three_kernel(tc, query, keys_words, keys_scales, note
         l5 = load_list("l5", offs5)
 
         f1 = sb.tile([P, POOL], F32, name="f1")
-        f2 = sb.tile([P, POOL], F32, name="f2")
         nc.vector.memset(f1[:], 0.0)
-        nc.vector.memset(f2[:], 0.0)
-        ident = sb.tile([P, P], F32, name="ident")
-        make_identity(nc, ident[:])
 
         q_bf = sb.tile([P, Q, 4], BF16, name="q_bf", align_bytes=64)
-        nc.vector.tensor_copy(out=q_bf[:].rearrange("p (c i) t -> p c t i", i=4),
-                              in_=q_raw[:].rearrange("p t (c i) -> p c t i", i=4))
         q_codes = sb.tile([P, Q], U32, name="q_codes", align_bytes=64)
         q_plane = sb.tile([P, Q], U8, name="q_plane", align_bytes=64)
-        nc.vector.quantize_mx(out=q_codes[:].bitcast(FP8X4), scales=q_plane[:], in_=q_bf[:].rearrange("p q t -> p (q t)"))
+        q_halves = (slice(0, Q // 2), slice(Q // 2, Q))
+        for s in q_halves:
+            nc.vector.tensor_copy(out=q_bf[:, s, :].rearrange("p (c i) t -> p c t i", i=4),
+                                  in_=q_raw[:, :, s].rearrange("p t (c i) -> p c t i", i=4))
+        for s in q_halves:
+            nc.vector.quantize_mx(out=q_codes[:, s].bitcast(FP8X4), scales=q_plane[:, s],
+                                  in_=q_bf[:, s, :].rearrange("p q t -> p (q t)"))
+
+        f2 = sb.tile([P, POOL], F32, name="q_raw")
+        nc.vector.memset(f2[:], 0.0)
+        ident = sb.tile([P, P], F32, name="q_bf", align_bytes=64)
+        make_identity(nc, ident[:])
 
         def score(tag, words, bytes_per_col, dtype, plane, x0, x1):
             bank = ps.tile([P, x1 - x0], F32, name=tag)
@@ -96,64 +101,68 @@ def tile_attend_twoerrands_three_kernel(tc, query, keys_words, keys_scales, note
         a = sb.tile([P, POOL], F32, name="a")
         b = sb.tile([P, POOL], F32, name="b")
         c0 = sb.tile([P, POOL], F32, name="c0")
-        b_cuts = (0, 512, 768, 1024)
-        b_ps = [score("b%d" % h, n_words, 2, FP4X4, n_plane, b_cuts[h], b_cuts[h + 1]) for h in range(3)]
-        a_ps = [score("a%d" % h, k_words, 1, FP8X4, k_plane, h * BANK, (h + 1) * BANK) for h in range(2)]
-        c_ps = [score("c%d" % h, u_words, 1, FP8X4, u_plane, h * BANK, (h + 1) * BANK) for h in range(2)]
+        W = 256
+        b_ps = [score("b%d" % h, n_words, 2, FP4X4, n_plane, h * W, (h + 1) * W) for h in range(4)]
+        a_ps = [score("s%d" % h, k_words, 1, FP8X4, k_plane, h * W, (h + 1) * W) for h in range(4)]
 
         hc = LIST_COLS // 2
-        nc.vector.tensor_copy(out=b[:, 0:512], in_=b_ps[0][:])
-        nc.scalar.activation(b[:, 512:768], b_ps[1][:], COPY)
-        nc.vector.tensor_copy(out=b[:, 768:1024], in_=b_ps[2][:])
+        for h in range(4):
+            if h % 2 == 0:
+                nc.scalar.activation(b[:, h * W:(h + 1) * W], b_ps[h][:], COPY)
+            else:
+                nc.vector.tensor_copy(out=b[:, h * W:(h + 1) * W], in_=b_ps[h][:])
         neg_b = sb.tile([P, SLOTS], F32, name="neg_b")
-        nc.vector.tensor_scalar(neg_b[:, :HALF], b[:].indirect(l2[:, :hc]), -1.0, 0.0, MULT, ADD)
-        nc.scalar.activation(neg_b[:, HALF:], b[:].indirect(l2[:, hc:]), COPY, scale=-1.0)
-        nc.vector.tensor_copy(out=a[:, cols(0)], in_=a_ps[0][:])
-        nc.scalar.activation(a[:, cols(1)], a_ps[1][:], COPY)
+        nc.scalar.activation(neg_b[:], b[:].indirect(l2[:]), COPY, scale=-1.0)
+        for h in range(4):
+            nc.vector.tensor_copy(out=a[:, h * W:(h + 1) * W], in_=a_ps[h][:])
+        c_ps = [score("s%d" % h, u_words, 1, FP8X4, u_plane, h * BANK, (h + 1) * BANK) for h in range(2)]
         a_at = sb.tile([P, SLOTS], F32, name="a_at")
+        neg_a = sb.tile([P, SLOTS], F32, name="neg_a")
         nc.vector.tensor_copy(out=a_at[:, :HALF], in_=a[:].indirect(l1[:, :hc]))
         nc.scalar.activation(a_at[:, HALF:], a[:].indirect(l1[:, hc:]), COPY)
+        nc.vector.tensor_scalar(neg_a[:, :HALF], a_at[:, :HALF], -1.0, None, MULT)
         nc.vector.tensor_tensor(f1[:].indirect(l3[:]), a_at[:], neg_b[:], ADD)
 
-        neg_a = sb.tile([P, SLOTS], F32, name="neg_a")
         for h in range(2):
             nc.scalar.activation(c0[:, cols(h)], c_ps[h][:], COPY)
-        nc.scalar.activation(neg_a[:], a_at[:], COPY, scale=-1.0)
+        nc.scalar.activation(neg_a[:, HALF:], a_at[:, HALF:], COPY, scale=-1.0)
         c_at = sb.tile([P, SLOTS], F32, name="c_at")
         nc.scalar.activation(c_at[:], c0[:].indirect(l3[:]), COPY)
         nc.vector.tensor_tensor(f2[:].indirect(l4[:]), c_at[:], neg_a[:], ADD)
 
-        turned = [ps.tile([P, BANK], F32, name="a%d" % h) for h in range(2)]
-        for h in range(2):
-            for j in range(4):
-                x0 = h * BANK + j * P
+        turned = [ps.tile([P, W], F32, name=tag) for tag in ("s2", "s3", "b3", "s0")]
+        for h in range(4):
+            for j in range(2):
+                x0 = h * W + j * P
                 nc.tensor.matmul(turned[h][:, j * P:(j + 1) * P], c0[:, x0:x0 + P], ident[:], start=(j == 0), stop=False,
                                  is_transpose=True)
         cc_t = sb.tile([P, POOL], F32, name="cc_t")
-        for h in range(2):
-            for j in range(4):
-                x0 = h * BANK + j * P
-                nc.tensor.matmul(turned[h][:, j * P:(j + 1) * P], f1[:, x0:x0 + P], ident[:], start=False, stop=(j == 3),
+        for h in range(4):
+            for j in range(2):
+                x0 = h * W + j * P
+                nc.tensor.matmul(turned[h][:, j * P:(j + 1) * P], f1[:, x0:x0 + P], ident[:], start=False, stop=(j == 1),
                                  is_transpose=True)
-            nc.scalar.activation(cc_t[:, cols(h)], turned[h][:], COPY)
+            nc.scalar.activation(cc_t[:, h * W:(h + 1) * W], turned[h][:], COPY)
         cc = sb.tile([P, POOL], F32, name="cc")
-        for h in range(2):
-            back = ps.tile([P, BANK], F32, name="c%d" % h)
-            for j in range(4):
-                x0 = h * BANK + j * P
+        for h, tag in enumerate(("s1", "s2", "s3", "b3")):
+            back = ps.tile([P, W], F32, name=tag)
+            for j in range(2):
+                x0 = h * W + j * P
                 nc.tensor.transpose(back[:, j * P:(j + 1) * P], cc_t[:, x0:x0 + P], ident[:])
-            nc.scalar.activation(cc[:, cols(h)], back[:], COPY)
+            nc.scalar.activation(cc[:, h * W:(h + 1) * W], back[:], COPY)
         cc_at = sb.tile([P, SLOTS], F32, name="cc_at")
         nc.scalar.activation(cc_at[:], cc[:].indirect(l6[:]), COPY)
 
         bb = sb.tile([P, POOL], F32, name="bb")
-        nc.vector.tensor_tensor(bb[:], b[:], f2[:], ADD)
-        bb_lo = sb.tile([P, HALF], F32, name="bb_lo")
-        bb_hi = sb.tile([P, HALF], F32, name="cc")
-        nc.vector.tensor_copy(out=bb_lo[:], in_=bb[:].indirect(l5[:, :hc]))
-        nc.scalar.activation(bb_hi[:], bb[:].indirect(l5[:, hc:]), COPY)
+        for h in range(3):
+            s = slice(h * W, (h + 1) * W)
+            nc.vector.tensor_tensor(bb[:, s], b_ps[h][:], f2[:, s], ADD)
+        nc.gpsimd.tensor_tensor(bb[:, 3 * W:], b[:, 3 * W:], f2[:, 3 * W:], ADD)
+        bb_at = sb.tile([P, SLOTS], F32, name="bb_at")
+        for h in range(2):
+            nc.vector.tensor_copy(out=bb_at[:, h * HALF:(h + 1) * HALF], in_=bb[:].indirect(l5[:, h * hc:(h + 1) * hc]))
         y = sb.tile([P, SLOTS], F32, name="y")
         for h in range(2):
             s = slice(h * HALF, (h + 1) * HALF)
-            nc.vector.tensor_tensor(y[:, s], (bb_lo, bb_hi)[h][:], cc_at[:, s], MAX)
+            nc.vector.tensor_tensor(y[:, s], bb_at[:, s], cc_at[:, s], MAX)
             nc.sync.dma_start(out=out[:, s], in_=y[:, s])

@@ -102,15 +102,16 @@ def tile_attend_twoerrands_three_kernel(tc, query, keys_words, keys_scales, note
         b = sb.tile([P, POOL], F32, name="b")
         c0 = sb.tile([P, POOL], F32, name="c0")
         W = 256
-        b_ps = [score("b%d" % h, n_words, 2, FP4X4, n_plane, h * W, (h + 1) * W) for h in range(4)]
+        b_cuts = (0, 512, 768, 896, 1024)
+        b_ps = [score("b%d" % h, n_words, 2, FP4X4, n_plane, b_cuts[h], b_cuts[h + 1]) for h in range(4)]
         a_ps = [score("s%d" % h, k_words, 1, FP8X4, k_plane, h * W, (h + 1) * W) for h in range(4)]
 
         hc = LIST_COLS // 2
         for h in range(4):
-            if h % 2 == 0:
-                nc.scalar.activation(b[:, h * W:(h + 1) * W], b_ps[h][:], COPY)
+            if h in (1, 2):
+                nc.scalar.activation(b[:, b_cuts[h]:b_cuts[h + 1]], b_ps[h][:], COPY)
             else:
-                nc.vector.tensor_copy(out=b[:, h * W:(h + 1) * W], in_=b_ps[h][:])
+                nc.vector.tensor_copy(out=b[:, b_cuts[h]:b_cuts[h + 1]], in_=b_ps[h][:])
         neg_b = sb.tile([P, SLOTS], F32, name="neg_b")
         nc.scalar.activation(neg_b[:], b[:].indirect(l2[:]), COPY, scale=-1.0)
         for h in range(4):
@@ -130,7 +131,7 @@ def tile_attend_twoerrands_three_kernel(tc, query, keys_words, keys_scales, note
         nc.scalar.activation(c_at[:], c0[:].indirect(l3[:]), COPY)
         nc.vector.tensor_tensor(f2[:].indirect(l4[:]), c_at[:], neg_a[:], ADD)
 
-        turned = [ps.tile([P, W], F32, name=tag) for tag in ("s2", "s3", "b3", "s0")]
+        turned = [ps.tile([P, W], F32, name=tag) for tag in ("s2", "s3", "b3", "b2")]
         for h in range(4):
             for j in range(2):
                 x0 = h * W + j * P
@@ -144,7 +145,7 @@ def tile_attend_twoerrands_three_kernel(tc, query, keys_words, keys_scales, note
                                  is_transpose=True)
             nc.scalar.activation(cc_t[:, h * W:(h + 1) * W], turned[h][:], COPY)
         cc = sb.tile([P, POOL], F32, name="cc")
-        for h, tag in enumerate(("s1", "s2", "s3", "b3")):
+        for h, tag in enumerate(("s0", "s1", "s2", "s3")):
             back = ps.tile([P, W], F32, name=tag)
             for j in range(2):
                 x0 = h * W + j * P
@@ -153,14 +154,14 @@ def tile_attend_twoerrands_three_kernel(tc, query, keys_words, keys_scales, note
         cc_at = sb.tile([P, SLOTS], F32, name="cc_at")
         nc.scalar.activation(cc_at[:], cc[:].indirect(l6[:]), COPY)
 
-        bb = sb.tile([P, POOL], F32, name="bb")
-        for h in range(3):
-            s = slice(h * W, (h + 1) * W)
+        bb = sb.tile([P, POOL], F32, name="cc_t")
+        for h in range(2):
+            s = slice(b_cuts[h], b_cuts[h + 1])
             nc.vector.tensor_tensor(bb[:, s], b_ps[h][:], f2[:, s], ADD)
         nc.gpsimd.tensor_tensor(bb[:, 3 * W:], b[:, 3 * W:], f2[:, 3 * W:], ADD)
         bb_at = sb.tile([P, SLOTS], F32, name="bb_at")
-        for h in range(2):
-            nc.vector.tensor_copy(out=bb_at[:, h * HALF:(h + 1) * HALF], in_=bb[:].indirect(l5[:, h * hc:(h + 1) * hc]))
+        nc.vector.tensor_copy(out=bb_at[:, :HALF], in_=bb[:].indirect(l5[:, :hc]))
+        nc.scalar.activation(bb_at[:, HALF:], bb[:].indirect(l5[:, hc:]), COPY)
         y = sb.tile([P, SLOTS], F32, name="y")
         for h in range(2):
             s = slice(h * HALF, (h + 1) * HALF)

@@ -37,10 +37,10 @@ def tile_attend_twoerrands_three_kernel(tc, query, keys_words, keys_scales, note
             nc.vector.memset(plane[:].bitcast(U32), 0)
             return plane
 
-        def load_plane(plane, scales):
+        def load_plane(plane, scales, queues):
             rows = scales[0].bitcast(I32)
             for r in range(4):
-                nc.sync.dma_start(out=plane[r:P:32, :].bitcast(I32), in_=rows[r:16:4, :])
+                queues[r].dma_start(out=plane[r:P:32, :].bitcast(I32), in_=rows[r:16:4, :])
 
         def load_list(name, src):
             t = lists.tile([P, LIST_COLS], U16, name=name)
@@ -54,16 +54,16 @@ def tile_attend_twoerrands_three_kernel(tc, query, keys_words, keys_scales, note
         q_raw = sb.tile([P, 4, Q], F32, name="q_raw")
         nc.sync.dma_start(out=q_raw[:], in_=query.rearrange("(p j) q -> p j q", j=4))
         l2 = load_list("l2", offs2)
-        load_plane(n_plane, notes_scales)
+        load_plane(n_plane, notes_scales, (nc.sync, nc.scalar, nc.sync, nc.scalar))
         n_words = sb.tile([P, 2 * POOL], U8, name="n_words", align_bytes=64)
         nc.sync.dma_start(out=n_words[:].bitcast(I32), in_=notes_words[0].bitcast(I32))
         k_words = sb.tile([P, POOL], U32, name="k_words", align_bytes=64)
         nc.sync.dma_start(out=k_words[:].bitcast(I32), in_=keys_words[0].rearrange("p n t -> p (n t)").bitcast(I32))
-        load_plane(k_plane, keys_scales)
+        load_plane(k_plane, keys_scales, (nc.sync,) * 4)
         u_words = sb.tile([P, POOL], U32, name="u_words", align_bytes=64)
         nc.sync.dma_start(out=u_words[:].bitcast(I32), in_=users_words[0].rearrange("p n t -> p (n t)").bitcast(I32))
         l1 = load_list("l1", offs)
-        load_plane(u_plane, users_scales)
+        load_plane(u_plane, users_scales, (nc.sync,) * 4)
         l3 = load_list("l3", offs3)
         l4 = load_list("l4", offs4)
         l6 = load_list("l6", offs6)

from contextlib import ExitStack

import concourse.mybir as mybir
from concourse.masks import make_identity

F32 = mybir.dt.float32
BF16 = mybir.dt.bfloat16
I32 = mybir.dt.int32
U32 = mybir.dt.uint32
U16 = mybir.dt.uint16
U8 = mybir.dt.uint8
FP8X4 = mybir.dt.float8_e4m3fn_x4
FP4X4 = mybir.dt.float4_e2m1fn_x4
ADD = mybir.AluOpType.add
MULT = mybir.AluOpType.mult
MAX = mybir.AluOpType.max
COPY = mybir.ActivationFunctionType.Copy

P = 128
D, POOL, SLOTS, Q = 512, 1024, 512, 128
BANK = 512
HALF = SLOTS // 2
LIST_COLS = SLOTS // 16
FLOPS = 3 * 2 * D * Q * POOL


def tile_attend_twoerrands_three_kernel(tc, query, keys_words, keys_scales, notes_words, notes_scales, users_words,
                                         users_scales, offs, offs2, offs3, offs4, offs5, offs6, out):
    nc = tc.nc
    with ExitStack() as ctx:
        lists = ctx.enter_context(tc.tile_pool(name="lists", bufs=1))
        sb = ctx.enter_context(tc.tile_pool(name="sb", bufs=1))
        ps = ctx.enter_context(tc.psum_pool(name="ps", bufs=1))

        def new_plane(name):
            plane = sb.tile([P, POOL], U8, name=name, align_bytes=64)
            nc.vector.memset(plane[:].bitcast(U32), 0)
            return plane

        def load_plane(plane, scales, queues):
            rows = scales[0].bitcast(I32)
            for r in range(4):
                queues[r].dma_start(out=plane[r:P:32, :].bitcast(I32), in_=rows[r:16:4, :])

        def load_list(name, src):
            t = lists.tile([P, LIST_COLS], U16, name=name)
            nc.sync.dma_start(t[:], src)
            return t

        n_plane = new_plane("n_plane")
        k_plane = new_plane("k_plane")
        u_plane = new_plane("u_plane")

        q_raw = sb.tile([P, 4, Q], F32, name="q_raw")
        nc.sync.dma_start(out=q_raw[:], in_=query.rearrange("(p j) q -> p j q", j=4))
        l2 = load_list("l2", offs2)
        load_plane(n_plane, notes_scales, (nc.sync, nc.scalar, nc.sync, nc.scalar))
        n_words = sb.tile([P, 2 * POOL], U8, name="n_words", align_bytes=64)
        nc.sync.dma_start(out=n_words[:].bitcast(I32), in_=notes_words[0].bitcast(I32))
        k_words = sb.tile([P, POOL], U32, name="k_words", align_bytes=64)
        nc.sync.dma_start(out=k_words[:].bitcast(I32), in_=keys_words[0].rearrange("p n t -> p (n t)").bitcast(I32))
        load_plane(k_plane, keys_scales, (nc.sync,) * 4)
        u_words = sb.tile([P, POOL], U32, name="u_words", align_bytes=64)
        nc.sync.dma_start(out=u_words[:].bitcast(I32), in_=users_words[0].rearrange("p n t -> p (n t)").bitcast(I32))
        l1 = load_list("l1", offs)
        load_plane(u_plane, users_scales, (nc.sync,) * 4)
        l3 = load_list("l3", offs3)
        l4 = load_list("l4", offs4)
        l6 = load_list("l6", offs6)
        l5 = load_list("l5", offs5)

        f1 = sb.tile([P, POOL], F32, name="f1")
        nc.vector.memset(f1[:], 0.0)

        q_bf = sb.tile([P, Q, 4], BF16, name="q_bf", align_bytes=64)
        q_codes = sb.tile([P, Q], U32, name="q_codes", align_bytes=64)
        q_plane = sb.tile([P, Q], U8, name="q_plane", align_bytes=64)
        q_halves = (slice(0, Q // 2), slice(Q // 2, Q))
        for s in q_halves:
            nc.vector.tensor_copy(out=q_bf[:, s, :].rearrange("p (c i) t -> p c t i", i=4),
                                  in_=q_raw[:, :, s].rearrange("p t (c i) -> p c t i", i=4))
        for s in q_halves:
            nc.vector.quantize_mx(out=q_codes[:, s].bitcast(FP8X4), scales=q_plane[:, s],
                                  in_=q_bf[:, s, :].rearrange("p q t -> p (q t)"))

        f2 = sb.tile([P, POOL], F32, name="q_raw")
        nc.vector.memset(f2[:], 0.0)
        ident = sb.tile([P, P], F32, name="q_bf", align_bytes=64)
        make_identity(nc, ident[:])

        def score(tag, words, bytes_per_col, dtype, plane, x0, x1):
            bank = ps.tile([P, x1 - x0], F32, name=tag)
            nc.tensor.matmul_mx(out=bank[:], lhsT=q_codes[:].bitcast(FP8X4), lhsT_scale=q_plane[:],
                                rhs=words[:, bytes_per_col * x0:bytes_per_col * x1].bitcast(dtype),
                                rhs_scale=plane[:, x0:x1], start=True, stop=True)
            return bank

        def cols(h):
            return slice(h * BANK, (h + 1) * BANK)

        a = sb.tile([P, POOL], F32, name="a")
        b = sb.tile([P, POOL], F32, name="b")
        c0 = sb.tile([P, POOL], F32, name="c0")
        W = 256
        b_cuts = (0, 512, 768, 896, 1024)
        b_ps = [score("b%d" % h, n_words, 2, FP4X4, n_plane, b_cuts[h], b_cuts[h + 1]) for h in range(4)]
        a_ps = [score("s%d" % h, k_words, 1, FP8X4, k_plane, h * W, (h + 1) * W) for h in range(4)]

        hc = LIST_COLS // 2
        for h in range(4):
            if h in (1, 2):
                nc.scalar.activation(b[:, b_cuts[h]:b_cuts[h + 1]], b_ps[h][:], COPY)
            else:
                nc.vector.tensor_copy(out=b[:, b_cuts[h]:b_cuts[h + 1]], in_=b_ps[h][:])
        neg_b = sb.tile([P, SLOTS], F32, name="neg_b")
        nc.scalar.activation(neg_b[:], b[:].indirect(l2[:]), COPY, scale=-1.0)
        for h in range(4):
            nc.vector.tensor_copy(out=a[:, h * W:(h + 1) * W], in_=a_ps[h][:])
        c_ps = [score("s%d" % h, u_words, 1, FP8X4, u_plane, h * BANK, (h + 1) * BANK) for h in range(2)]
        a_at = sb.tile([P, SLOTS], F32, name="a_at")
        neg_a = sb.tile([P, SLOTS], F32, name="neg_a")
        nc.vector.tensor_copy(out=a_at[:, :HALF], in_=a[:].indirect(l1[:, :hc]))
        nc.scalar.activation(a_at[:, HALF:], a[:].indirect(l1[:, hc:]), COPY)
        nc.vector.tensor_scalar(neg_a[:, :HALF], a_at[:, :HALF], -1.0, None, MULT)
        nc.vector.tensor_tensor(f1[:].indirect(l3[:]), a_at[:], neg_b[:], ADD)

        for h in range(2):
            nc.scalar.activation(c0[:, cols(h)], c_ps[h][:], COPY)
        nc.scalar.activation(neg_a[:, HALF:], a_at[:, HALF:], COPY, scale=-1.0)
        c_at = sb.tile([P, SLOTS], F32, name="c_at")
        nc.scalar.activation(c_at[:], c0[:].indirect(l3[:]), COPY)
        nc.vector.tensor_tensor(f2[:].indirect(l4[:]), c_at[:], neg_a[:], ADD)

        turned = [ps.tile([P, W], F32, name=tag) for tag in ("s2", "s3", "b3", "b2")]
        for h in range(4):
            for j in range(2):
                x0 = h * W + j * P
                nc.tensor.matmul(turned[h][:, j * P:(j + 1) * P], c0[:, x0:x0 + P], ident[:], start=(j == 0), stop=False,
                                 is_transpose=True)
        cc_t = sb.tile([P, POOL], F32, name="cc_t")
        for h in range(4):
            for j in range(2):
                x0 = h * W + j * P
                nc.tensor.matmul(turned[h][:, j * P:(j + 1) * P], f1[:, x0:x0 + P], ident[:], start=False, stop=(j == 1),
                                 is_transpose=True)
            nc.scalar.activation(cc_t[:, h * W:(h + 1) * W], turned[h][:], COPY)
        cc = sb.tile([P, POOL], F32, name="cc")
        for h, tag in enumerate(("s0", "s1", "s2", "s3")):
            back = ps.tile([P, W], F32, name=tag)
            for j in range(2):
                x0 = h * W + j * P
                nc.tensor.transpose(back[:, j * P:(j + 1) * P], cc_t[:, x0:x0 + P], ident[:])
            nc.scalar.activation(cc[:, h * W:(h + 1) * W], back[:], COPY)
        cc_at = sb.tile([P, SLOTS], F32, name="cc_at")
        nc.scalar.activation(cc_at[:], cc[:].indirect(l6[:]), COPY)

        bb = sb.tile([P, POOL], F32, name="cc_t")
        for h in range(2):
            s = slice(b_cuts[h], b_cuts[h + 1])
            nc.vector.tensor_tensor(bb[:, s], b_ps[h][:], f2[:, s], ADD)
        nc.gpsimd.tensor_tensor(bb[:, 3 * W:], b[:, 3 * W:], f2[:, 3 * W:], ADD)
        bb_at = sb.tile([P, SLOTS], F32, name="bb_at")
        nc.vector.tensor_copy(out=bb_at[:, :HALF], in_=bb[:].indirect(l5[:, :hc]))
        nc.scalar.activation(bb_at[:, HALF:], bb[:].indirect(l5[:, hc:]), COPY)
        y = sb.tile([P, SLOTS], F32, name="y")
        for h in range(2):
            s = slice(h * HALF, (h + 1) * HALF)
            nc.vector.tensor_tensor(y[:, s], bb_at[:, s], cc_at[:, s], MAX)
            nc.sync.dma_start(out=out[:, s], in_=y[:, s])
